import numpy as np
import ml_dtypes


def mxq(x, axis, fmt="e4m3"):
    dtype, down = {"e4m3": (ml_dtypes.float8_e4m3fn, 7), "e5m2": (ml_dtypes.float8_e5m2, 14)}[fmt]
    v = np.moveaxis(np.asarray(x, np.float32).astype(ml_dtypes.bfloat16).astype(np.float64), axis, -1)
    blocks = v.reshape(v.shape[:-1] + (-1, 32))
    amax = np.abs(blocks).max(-1, keepdims=True)
    byte = np.maximum(np.where(amax > 0, np.frexp(amax)[1] - 1 + 127, 0) - down, 1)
    scale = np.exp2(byte - 127.0)
    codes = (blocks / scale).astype(np.float32).astype(dtype).astype(np.float64)
    return np.moveaxis((codes * scale).reshape(v.shape), -1, axis)


WIDE = False


def mx_kscale(k):
    if not WIDE:
        return np.ones(k)
    levels = np.array([10, -10, 5, -5, 0])
    if k % 512:
        return np.exp2(np.random.permutation(np.resize(levels, k // 32))).repeat(32)
    a = np.empty((k // 512, 16))
    for p in range(k // 512):
        a[p, :8] = np.random.permutation(np.resize(levels, 8))
        for g in range(8):
            far = levels[np.abs(levels - a[p, g]) >= 10]
            a[p, g + 8] = far[np.random.randint(len(far))]
    return np.exp2(a.ravel()).repeat(32)


def f64(x):
    return np.asarray(x).astype(np.float64)


def striped(idx):
    return np.tile(idx.reshape(-1, 16).T, (8, 1)).astype(np.uint16)


def unstriped(offs):
    return offs[:16].T.reshape(-1).astype(np.int64)


def pack_weight(w):
    k, n = w.shape
    w = f64(np.asarray(w, np.float32).astype(ml_dtypes.bfloat16)).reshape(k // 32, 32, n)
    amax = np.abs(w).max(1)
    byte = np.clip(np.where(amax > 0, np.frexp(amax)[1] - 1 + 127 - 7, 1), 1, 254)
    scaled = (w * np.exp2(127.0 - byte)[:, None, :]).reshape(k, n).astype(np.float32)
    words = np.ascontiguousarray(scaled.reshape(k // 512, 128, 4, n).transpose(0, 1, 3, 2)).astype(ml_dtypes.float8_e4m3fn).view(np.uint8)
    return words, np.ascontiguousarray(byte.astype(np.uint8).reshape(k // 512, 16, n))


def unpack_weight(words, scales):
    g, p, n, _ = words.shape
    vals = np.ascontiguousarray(words).view(ml_dtypes.float8_e4m3fn).astype(np.float64) * np.repeat(np.exp2(scales.astype(np.float64) - 127.0), 8, axis=1)[..., None]
    return vals.transpose(0, 1, 3, 2).reshape(g * 512, n)


def relu(v):
    return np.maximum(v, 0.0)


K, T, S, H, N, U, V = 512, 2048, 1024, 512, 256, 1024, 512


def setup_inputs():
    n = np.random.standard_normal
    s = mx_kscale(K)[:, None]
    u = mx_kscale(H)
    packed_xT = pack_weight(n((K, T)) * s)
    packed_w3 = pack_weight(n((H, N)) / np.sqrt(H) / u[:, None])
    return {
        "x_words": packed_xT[0],
        "x_scales": packed_xT[1],
        "w1": (n((K, H)) / np.sqrt(K) / s * u).astype(np.float32),
        "w2": (n((K, H)) / np.sqrt(K) / s * u).astype(np.float32),
        "w3_words": packed_w3[0],
        "w3_scales": packed_w3[1],
        "offs": striped(np.random.permutation(T)[:S]),
        "near": striped(np.random.permutation(U)[:V]),
        "far": striped(np.random.permutation(U)[:V]),
    }


def reference(x_words, x_scales, w1, w2, w3_words, w3_scales, offs, near, far):
    xq = unpack_weight(x_words, x_scales)[:, unstriped(offs)]
    a = np.zeros((H, S))
    a[:, unstriped(near)] = relu(mxq(f64(w1), 0, "e4m3").T @ xq[:, :V])
    e = np.zeros((H, S))
    e[:, unstriped(far)] = relu(mxq(f64(w2), 0, "e4m3").T @ xq[:, V:2 * V])
    z = np.maximum(a, e)
    return unpack_weight(w3_words, w3_scales).T @ mxq(z, 0, "e4m3")

@@ -1,0 +1,217 @@
+from contextlib import ExitStack
+
+import concourse.mybir as mybir
+
+K, T, H, N, CELLS, V = 512, 2048, 512, 256, 1024, 512
+FLOPS = 2 * (2 * K * H * V + H * N * CELLS)
+
+F32 = mybir.dt.float32
+BF16 = mybir.dt.bfloat16
+I32 = mybir.dt.int32
+U32 = mybir.dt.uint32
+U16 = mybir.dt.uint16
+U8 = mybir.dt.uint8
+FP8X4 = mybir.dt.float8_e4m3fn_x4
+RELU = mybir.ActivationFunctionType.Relu
+ALU = mybir.AluOpType
+
+P = 128
+PACK = 4
+QUAD = 32
+LIST_ROWS = 16
+CELL_CHUNKS = (256, 256, 256, 128, 128)
+
+
+def load_scale_rows(nc, plane, rows):
+    for q in range(P // QUAD):
+        nc.sync.dma_start(
+            out=plane[QUAD * q : QUAD * q + PACK, :].bitcast(I32),
+            in_=rows[PACK * q : PACK * (q + 1), :].bitcast(I32),
+        )
+
+
+def tile_picked_bev_max_p_kernel(
+    tc, x_words, x_scales, w1, w2, w3_words, w3_scales, offs, near, far, out
+):
+    nc = tc.nc
+    with ExitStack() as ctx:
+        keep = ctx.enter_context(tc.tile_pool(name="keep", bufs=1))
+        layer_psum = ctx.enter_context(tc.psum_pool(name="layer_psum", bufs=4))
+        out_psum = ctx.enter_context(tc.psum_pool(name="out_psum", bufs=4))
+
+        offs_sb = keep.tile([P, 2 * V // LIST_ROWS], U16)
+        near_sb = keep.tile([P, V // LIST_ROWS], U16)
+        far_sb = keep.tile([P, V // LIST_ROWS], U16)
+
+        x_plane = keep.tile([P, T], U8, align_bytes=64)
+        x_table = keep.tile([P, T], I32, align_bytes=64)
+        w3_plane = keep.tile([P, N], U8, align_bytes=64)
+        w3_codes = keep.tile([P, N], I32, align_bytes=64)
+        w1_spans = ((0, P), (P, 2 * P), (2 * P, H))
+        w1_raw = [keep.tile([P, PACK, hi - lo], F32, name="w1_raw%d" % s) for s, (lo, hi) in enumerate(w1_spans)]
+        w2_raw = keep.tile([P, PACK, H], F32)
+
+        near_windows = [keep.tile([P, 2 * CELLS], F32, align_bytes=64, name="near_window%d" % s) for s in range(3)]
+        far_windows = [keep.tile([P, CELLS + V], F32, name="far_window%d" % s) for s in range(2)]
+        left = keep.tile([P, PACK * CELLS], F32)
+        right = keep.tile([P, PACK * CELLS], F32)
+        zeros = keep.tile([P, V], F32)
+
+        nc.vector.memset(x_plane[:].bitcast(I32), 0)
+        nc.vector.memset(far_windows[0][:, :CELLS], 0.0)
+        nc.vector.memset(near_windows[0][:, :CELLS], 0.0)
+        nc.vector.memset(near_windows[1][:, :CELLS], 0.0)
+        nc.vector.memset(w3_plane[:].bitcast(I32), 0)
+        for cleared in (near_windows[2][:, :CELLS], far_windows[1][:, :CELLS], left[:, :CELLS]):
+            nc.scalar.copy(out=cleared, in_=far_windows[0][:, :CELLS])
+        nc.scalar.copy(out=zeros[:], in_=far_windows[0][:, :V])
+
+        nc.sync.dma_start(offs_sb[:], offs)
+        nc.sync.dma_start(near_sb[:], near)
+        nc.sync.dma_start(far_sb[:], far)
+        load_scale_rows(nc, x_plane, x_scales[0])
+        nc.sync.dma_start(out=x_table[:], in_=x_words[0].rearrange("p n t -> p (n t)").bitcast(I32))
+        w1_rows = w1.rearrange("(p j) c -> p j c", j=PACK)
+        for s, (lo, hi) in enumerate(w1_spans):
+            nc.sync.dma_start(out=w1_raw[s][:], in_=w1_rows[:, :, lo:hi])
+        nc.sync.dma_start(out=w2_raw[:], in_=w2.rearrange("(p j) c -> p j c", j=PACK))
+        nc.sync.dma_start(out=w3_codes[:], in_=w3_words[0].rearrange("p n t -> p (n t)").bitcast(I32))
+        load_scale_rows(nc, w3_plane, w3_scales[0])
+
+        picked_bytes = keep.tile([P, 2 * V], U8, align_bytes=64)
+        nc.vector.tensor_copy(picked_bytes[:], x_plane[:].indirect(offs_sb[:]))
+
+        def pick_words(sensor, tag):
+            words = keep.tile([P, V], U32, align_bytes=64, name="picked_words%d" % sensor, tag=tag)
+            cols = V // LIST_ROWS
+            nc.vector.tensor_copy(
+                words[:], x_table[:].bitcast(U32).indirect(offs_sb[:, sensor * cols : (sensor + 1) * cols])
+            )
+            return words
+
+        def quantise(name, grouped, width):
+            codes = keep.tile([P, width], U32, align_bytes=64, name=name + "_codes")
+            plane = keep.tile([P, width], U8, align_bytes=64, name=name + "_plane")
+            nc.vector.quantize_mx(out=codes[:].bitcast(FP8X4), scales=plane[:], in_=grouped)
+            return codes, plane
+
+        def round_w1(s, grouped):
+            nc.scalar.copy(
+                out=grouped.rearrange("p (c i j) -> p c j i", i=PACK, j=PACK),
+                in_=w1_raw[s][:].rearrange("p j (c i) -> p c j i", i=PACK),
+            )
+
+        def spare(window, width):
+            return window[:, CELLS : CELLS + width * PACK // 2].bitcast(BF16)
+
+        def layer_tile(hidden, weights, col, words, sensor):
+            codes, plane = weights
+            acc = layer_psum.tile([P, V], F32, tag="layer")
+            nc.tensor.matmul_mx(
+                out=acc[:],
+                lhsT=codes[:, col : col + P].bitcast(FP8X4),
+                lhsT_scale=plane[:, col : col + P],
+                rhs=words[:].bitcast(FP8X4),
+                rhs_scale=picked_bytes[:, sensor * V : (sensor + 1) * V],
+                start=True,
+                stop=True,
+            )
+            nc.scalar.activation(out=hidden, in_=acc[:], func=RELU)
+
+        def own_tile(name):
+            return keep.tile([P, V], F32, name=name)[:]
+
+        def near_tile(g, hidden, weights, col):
+            layer_tile(hidden, weights, col, near_words, 0)
+            window = near_windows[g % len(near_windows)]
+            nc.vector.tensor_copy(window[:].indirect(near_sb[:]), hidden)
+            for t in range(PACK):
+                side = right if t == 0 else left
+                nc.sync.dma_start(
+                    out=side[QUAD * g : QUAD * (g + 1), t * CELLS : (t + 1) * CELLS],
+                    in_=window[t:P:PACK, :CELLS],
+                )
+
+        near_words = pick_words(0, "near_words")
+        first_grouped = keep.tile([P, PACK * P], BF16, align_bytes=64, tag="first_grouped")
+        round_w1(0, first_grouped[:])
+        w1_first = quantise("w1_first", first_grouped[:], P)
+        far_words = pick_words(1, "first_grouped")
+
+        round_w1(1, spare(near_windows[0], P))
+        w1_second = quantise("w1_second", spare(near_windows[0], P), P)
+        near_tile(0, own_tile("near_hidden0"), w1_first, 0)
+
+        round_w1(2, spare(near_windows[1], 2 * P))
+        w1_rest = quantise("w1_rest", spare(near_windows[1], 2 * P), 2 * P)
+        near_tile(1, own_tile("near_hidden1"), w1_second, 0)
+
+        w2_grouped = spare(near_windows[2], H)
+        half = P // 2
+        for lo in (0, half):
+            nc.scalar.copy(
+                out=w2_grouped.rearrange("p (t m j) -> p m j t", t=PACK, j=PACK)[:, lo : lo + half],
+                in_=w2_raw[:].rearrange("p j (m t) -> p m j t", t=PACK)[:, lo : lo + half],
+            )
+        w2_mx = quantise("w2", w2_grouped, H)
+        near_tile(2, own_tile("near_hidden2"), w1_rest, 0)
+        near_tile(3, far_windows[1][:, CELLS:], w1_rest, P)
+
+        far_hidden = {
+            1: far_windows[0][:, CELLS:],
+            2: own_tile("far_hidden_shared"),
+            3: own_tile("far_hidden3"),
+        }
+        for t in (1, 2, 3):
+            layer_tile(far_hidden[t], w2_mx, t * P, far_words, 1)
+
+        def far_tile(t):
+            window = far_windows[t % len(far_windows)]
+            nc.vector.tensor_copy(window[:].indirect(far_sb[:]), far_hidden[t])
+            nc.scalar.copy(out=right[:, t * CELLS : (t + 1) * CELLS], in_=window[:, :CELLS])
+
+        far_tile(1)
+        far_tile(2)
+        far_hidden[0] = own_tile("far_hidden_shared")
+        layer_tile(far_hidden[0], w2_mx, 0, far_words, 1)
+        far_tile(3)
+        nc.vector.tensor_tensor(left[:].indirect(far_sb[:]), far_hidden[0], zeros[:], ALU.add)
+
+        out_rows = out.rearrange("(m p) c -> p m c", p=P)
+        starts = [sum(CELL_CHUNKS[:n]) for n in range(len(CELL_CHUNKS))]
+
+        def join(n):
+            lo, width = starts[n], CELL_CHUNKS[n]
+            grouped = keep.tile([P, PACK * width], BF16, align_bytes=64, name="z_grouped%d" % n)
+            pairs = slice(lo // 2, (lo + width) // 2)
+            nc.vector.tensor_tensor(
+                grouped[:].rearrange("p (c i t) -> p c t i", i=2, t=PACK),
+                left[:].rearrange("p (t c i) -> p c t i", t=PACK, i=2)[:, pairs],
+                right[:].rearrange("p (t c i) -> p c t i", t=PACK, i=2)[:, pairs],
+                ALU.max,
+            )
+            return grouped
+
+        def last_layer(n, grouped):
+            lo, width = starts[n], CELL_CHUNKS[n]
+            codes, plane = quantise("z%d" % n, grouped[:], width)
+            acc = out_psum.tile([P, N // P, width], F32, tag="last")
+            for m in range(N // P):
+                nc.tensor.matmul_mx(
+                    out=acc[:, m, :],
+                    lhsT=w3_codes[:, m * P : (m + 1) * P].bitcast(FP8X4),
+                    lhsT_scale=w3_plane[:, m * P : (m + 1) * P],
+                    rhs=codes[:].bitcast(FP8X4),
+                    rhs_scale=plane[:],
+                    start=True,
+                    stop=True,
+                )
+            result = keep.tile([P, N // P, width], F32, name="result%d" % n)
+            nc.scalar.copy(out=result[:], in_=acc[:])
+            nc.sync.dma_start(out=out_rows[:, :, lo : lo + width], in_=result[:])
+
+        joined = [join(0)]
+        for n in range(1, len(CELL_CHUNKS)):
+            joined.append(join(n))
+            last_layer(n - 1, joined[n - 1])
+        last_layer(len(CELL_CHUNKS) - 1, joined[-1])

@@ -53,18 +53,22 @@ def tile_picked_bev_max_p_kernel(
 
         near_windows = [keep.tile([P, 2 * CELLS], F32, align_bytes=64, name="near_window%d" % s) for s in range(3)]
         far_windows = [keep.tile([P, CELLS + V], F32, name="far_window%d" % s) for s in range(2)]
-        left = keep.tile([P, PACK * CELLS], F32)
-        right = keep.tile([P, PACK * CELLS], F32)
-        zeros = keep.tile([P, V], F32)
+        last_window = keep.tile([P, 2 * CELLS], F32)
+        last_partner = keep.tile([P, 2 * CELLS], F32)
+        near_pair = keep.tile([P, 2 * CELLS], F32)
+        far_pair = keep.tile([P, 2 * CELLS], F32)
+        near_plane = (
+            last_partner[:, :CELLS], last_window[:, CELLS:], near_pair[:, :CELLS], near_pair[:, CELLS:]
+        )
+        far_plane = (None, last_partner[:, CELLS:], far_pair[:, :CELLS], far_pair[:, CELLS:])
 
         nc.vector.memset(x_plane[:].bitcast(I32), 0)
         nc.vector.memset(far_windows[0][:, :CELLS], 0.0)
         nc.vector.memset(near_windows[0][:, :CELLS], 0.0)
         nc.vector.memset(near_windows[1][:, :CELLS], 0.0)
         nc.vector.memset(w3_plane[:].bitcast(I32), 0)
-        for cleared in (near_windows[2][:, :CELLS], far_windows[1][:, :CELLS], left[:, :CELLS]):
-            nc.scalar.copy(out=cleared, in_=far_windows[0][:, :CELLS])
-        nc.scalar.copy(out=zeros[:], in_=far_windows[0][:, :V])
+        for cleared in (near_windows[2][:, :CELLS], far_windows[1][:, :CELLS], last_window[:, :CELLS]):
+            nc.scalar.activation(out=cleared, in_=far_windows[0][:, :CELLS], func=RELU)
 
         nc.sync.dma_start(offs_sb[:], offs)
         nc.sync.dma_start(near_sb[:], near)
@@ -125,12 +129,8 @@ def tile_picked_bev_max_p_kernel(
             layer_tile(hidden, weights, col, near_words, 0)
             window = near_windows[g % len(near_windows)]
             nc.vector.tensor_copy(window[:].indirect(near_sb[:]), hidden)
-            for t in range(PACK):
-                side = right if t == 0 else left
-                nc.sync.dma_start(
-                    out=side[QUAD * g : QUAD * (g + 1), t * CELLS : (t + 1) * CELLS],
-                    in_=window[t:P:PACK, :CELLS],
-                )
+            for t in (3, 2, 0, 1):
+                nc.sync.dma_start(out=near_plane[t][QUAD * g : QUAD * (g + 1), :], in_=window[t:P:PACK, :CELLS])
 
         near_words = pick_words(0, "near_words")
         first_grouped = keep.tile([P, PACK * P], BF16, align_bytes=64, tag="first_grouped")
@@ -146,7 +146,9 @@ def tile_picked_bev_max_p_kernel(
         w1_rest = quantise("w1_rest", spare(near_windows[1], 2 * P), 2 * P)
         near_tile(1, own_tile("near_hidden1"), w1_second, 0)
 
-        w2_grouped = spare(near_windows[2], H)
+        near_tile(2, own_tile("near_hidden2"), w1_rest, 0)
+
+        w2_grouped = spare(near_windows[0], H)
         half = P // 2
         for lo in (0, half):
             nc.scalar.copy(
@@ -154,41 +156,53 @@ def tile_picked_bev_max_p_kernel(
                 in_=w2_raw[:].rearrange("p j (m t) -> p m j t", t=PACK)[:, lo : lo + half],
             )
         w2_mx = quantise("w2", w2_grouped, H)
-        near_tile(2, own_tile("near_hidden2"), w1_rest, 0)
         near_tile(3, far_windows[1][:, CELLS:], w1_rest, P)
 
         far_hidden = {
-            1: far_windows[0][:, CELLS:],
-            2: own_tile("far_hidden_shared"),
-            3: own_tile("far_hidden3"),
+            3: far_windows[0][:, CELLS:],
+            2: own_tile("far_hidden2"),
+            1: own_tile("far_hidden_shared"),
         }
-        for t in (1, 2, 3):
+        for t in (3, 2, 1):
             layer_tile(far_hidden[t], w2_mx, t * P, far_words, 1)
 
-        def far_tile(t):
-            window = far_windows[t % len(far_windows)]
-            nc.vector.tensor_copy(window[:].indirect(far_sb[:]), far_hidden[t])
-            nc.scalar.copy(out=right[:, t * CELLS : (t + 1) * CELLS], in_=window[:, :CELLS])
+        def scatter_far(t):
+            nc.vector.tensor_copy(far_windows[t % 2][:].indirect(far_sb[:]), far_hidden[t])
 
-        far_tile(1)
-        far_tile(2)
+        def place_far(t):
+            nc.scalar.copy(out=far_plane[t], in_=far_windows[t % 2][:, :CELLS])
+
+        starts = [sum(CELL_CHUNKS[:n]) for n in range(len(CELL_CHUNKS))]
+        pairs = [keep.tile([P, 2, 2 * width], BF16, name="pairs%d" % n) for n, width in enumerate(CELL_CHUNKS)]
+
+        def join(n, u, one, other):
+            cells = slice(starts[n], starts[n] + CELL_CHUNKS[n])
+            nc.vector.tensor_tensor(
+                pairs[n][:, u, :].rearrange("p (c e) -> p c e", e=2),
+                one[:].rearrange("p (e c) -> p c e", e=2)[:, cells],
+                other[:].rearrange("p (e c) -> p c e", e=2)[:, cells],
+                ALU.max,
+            )
+
+        for t in (3, 2):
+            scatter_far(t)
+            place_far(t)
+        scatter_far(1)
         far_hidden[0] = own_tile("far_hidden_shared")
         layer_tile(far_hidden[0], w2_mx, 0, far_words, 1)
-        far_tile(3)
-        nc.vector.tensor_tensor(left[:].indirect(far_sb[:]), far_hidden[0], zeros[:], ALU.add)
+        place_far(1)
+        for n in range(len(CELL_CHUNKS)):
+            join(n, 1, far_pair, near_pair)
+        nc.vector.tensor_copy(last_window[:].indirect(far_sb[:]), far_hidden[0])
 
         out_rows = out.rearrange("(m p) c -> p m c", p=P)
-        starts = [sum(CELL_CHUNKS[:n]) for n in range(len(CELL_CHUNKS))]
 
-        def join(n):
-            lo, width = starts[n], CELL_CHUNKS[n]
-            grouped = keep.tile([P, PACK * width], BF16, align_bytes=64, name="z_grouped%d" % n)
-            pairs = slice(lo // 2, (lo + width) // 2)
-            nc.vector.tensor_tensor(
-                grouped[:].rearrange("p (c i t) -> p c t i", i=2, t=PACK),
-                left[:].rearrange("p (t c i) -> p c t i", t=PACK, i=2)[:, pairs],
-                right[:].rearrange("p (t c i) -> p c t i", t=PACK, i=2)[:, pairs],
-                ALU.max,
+        def weave(n):
+            join(n, 0, last_window, last_partner)
+            grouped = keep.tile([P, PACK * CELL_CHUNKS[n]], BF16, align_bytes=64, name="z_grouped%d" % n)
+            nc.scalar.copy(
+                out=grouped[:].bitcast(F32).rearrange("p (c u) -> p c u", u=2),
+                in_=pairs[n][:].bitcast(F32).rearrange("p u c -> p c u"),
             )
             return grouped
 
@@ -206,12 +220,23 @@ def tile_picked_bev_max_p_kernel(
                     start=True,
                     stop=True,
                 )
+            return acc
+
+        def store(n, acc):
+            lo, width = starts[n], CELL_CHUNKS[n]
             result = keep.tile([P, N // P, width], F32, name="result%d" % n)
-            nc.scalar.copy(out=result[:], in_=acc[:])
+            if n % 2 == 0:
+                nc.scalar.copy(out=result[:], in_=acc[:])
+            else:
+                nc.vector.tensor_copy(out=result[:], in_=acc[:])
             nc.sync.dma_start(out=out_rows[:, :, lo : lo + width], in_=result[:])
 
-        joined = [join(0)]
-        for n in range(1, len(CELL_CHUNKS)):
-            joined.append(join(n))
-            last_layer(n - 1, joined[n - 1])
-        last_layer(len(CELL_CHUNKS) - 1, joined[-1])
+        count = len(CELL_CHUNKS)
+        woven, sums = {}, {}
+        for step in range(count + 3):
+            if step < count:
+                woven[step] = weave(step)
+            if 0 <= step - 2 < count:
+                sums[step - 2] = last_layer(step - 2, woven[step - 2])
+            if 0 <= step - 3 < count:
+                store(step - 3, sums[step - 3])

@@ -56,18 +56,16 @@ def tile_picked_bev_max_p_kernel(
         last_window = keep.tile([P, 2 * CELLS], F32)
         last_partner = keep.tile([P, 2 * CELLS], F32)
         near_pair = keep.tile([P, 2 * CELLS], F32)
-        far_pair = keep.tile([P, 2 * CELLS], F32)
         near_plane = (
-            last_partner[:, :CELLS], last_window[:, CELLS:], near_pair[:, :CELLS], near_pair[:, CELLS:]
+            last_partner[:, CELLS:], last_window[:, CELLS:], near_pair[:, :CELLS], near_pair[:, CELLS:]
         )
-        far_plane = (None, last_partner[:, CELLS:], far_pair[:, :CELLS], far_pair[:, CELLS:])
 
         nc.vector.memset(x_plane[:].bitcast(I32), 0)
         nc.vector.memset(far_windows[0][:, :CELLS], 0.0)
         nc.vector.memset(near_windows[0][:, :CELLS], 0.0)
         nc.vector.memset(near_windows[1][:, :CELLS], 0.0)
         nc.vector.memset(w3_plane[:].bitcast(I32), 0)
-        for cleared in (near_windows[2][:, :CELLS], far_windows[1][:, :CELLS], last_window[:, :CELLS]):
+        for cleared in (near_windows[2][:, :CELLS], far_windows[1][:, :CELLS], last_partner[:, :CELLS], last_window[:, :CELLS]):
             nc.scalar.activation(out=cleared, in_=far_windows[0][:, :CELLS], func=RELU)
 
         nc.sync.dma_start(offs_sb[:], offs)
@@ -158,51 +156,46 @@ def tile_picked_bev_max_p_kernel(
         w2_mx = quantise("w2", w2_grouped, H)
         near_tile(3, far_windows[1][:, CELLS:], w1_rest, P)
 
-        far_hidden = {
-            3: far_windows[0][:, CELLS:],
-            2: own_tile("far_hidden2"),
-            1: own_tile("far_hidden_shared"),
-        }
-        for t in (3, 2, 1):
+        far_hidden = {3: far_windows[0][:, CELLS:]}
+        for t in (2, 1, 0):
+            far_hidden[t] = own_tile("far_hidden%d" % t)
+        for t in (3, 2, 1, 0):
             layer_tile(far_hidden[t], w2_mx, t * P, far_words, 1)
 
-        def scatter_far(t):
-            nc.vector.tensor_copy(far_windows[t % 2][:].indirect(far_sb[:]), far_hidden[t])
-
-        def place_far(t):
-            nc.scalar.copy(out=far_plane[t], in_=far_windows[t % 2][:, :CELLS])
-
         starts = [sum(CELL_CHUNKS[:n]) for n in range(len(CELL_CHUNKS))]
-        pairs = [keep.tile([P, 2, 2 * width], BF16, name="pairs%d" % n) for n, width in enumerate(CELL_CHUNKS)]
+        pairs = keep.tile([P, PACK * CELLS], BF16)
+        pair_view = pairs[:].rearrange("p (u c e) -> p u c e", u=2, e=2)
 
-        def join(n, u, one, other):
-            cells = slice(starts[n], starts[n] + CELL_CHUNKS[n])
-            nc.vector.tensor_tensor(
-                pairs[n][:, u, :].rearrange("p (c e) -> p c e", e=2),
-                one[:].rearrange("p (e c) -> p c e", e=2)[:, cells],
-                other[:].rearrange("p (e c) -> p c e", e=2)[:, cells],
-                ALU.max,
-            )
-
+        halves = (slice(0, CELLS // 2), slice(CELLS // 2, CELLS))
         for t in (3, 2):
-            scatter_far(t)
-            place_far(t)
-        scatter_far(1)
-        far_hidden[0] = own_tile("far_hidden_shared")
-        layer_tile(far_hidden[0], w2_mx, 0, far_words, 1)
-        place_far(1)
-        for n in range(len(CELL_CHUNKS)):
-            join(n, 1, far_pair, near_pair)
+            window = far_windows[t % 2]
+            nc.vector.tensor_copy(window[:].indirect(far_sb[:]), far_hidden[t])
+            difference = keep.tile([P, CELLS], F32, name="difference%d" % t)
+            excess = keep.tile([P, CELLS], F32, name="excess%d" % t)
+            for cells in halves:
+                nc.gpsimd.tensor_tensor(difference[:, cells], window[:, cells], near_plane[t][:, cells], ALU.subtract)
+                nc.scalar.activation(out=excess[:, cells], in_=difference[:, cells], func=RELU)
+            for cells in halves:
+                nc.gpsimd.tensor_tensor(
+                    pair_view[:, 1, cells, t % 2], near_plane[t][:, cells], excess[:, cells], ALU.add
+                )
+        nc.vector.tensor_copy(last_partner[:].indirect(far_sb[:]), far_hidden[1])
         nc.vector.tensor_copy(last_window[:].indirect(far_sb[:]), far_hidden[0])
 
         out_rows = out.rearrange("(m p) c -> p m c", p=P)
 
         def weave(n):
-            join(n, 0, last_window, last_partner)
+            cells = slice(starts[n], starts[n] + CELL_CHUNKS[n])
+            nc.vector.tensor_tensor(
+                pair_view[:, 0, cells, :],
+                last_window[:].rearrange("p (e c) -> p c e", e=2)[:, cells, :],
+                last_partner[:].rearrange("p (e c) -> p c e", e=2)[:, cells, ::-1],
+                ALU.max,
+            )
             grouped = keep.tile([P, PACK * CELL_CHUNKS[n]], BF16, align_bytes=64, name="z_grouped%d" % n)
             nc.scalar.copy(
                 out=grouped[:].bitcast(F32).rearrange("p (c u) -> p c u", u=2),
-                in_=pairs[n][:].bitcast(F32).rearrange("p u c -> p c u"),
+                in_=pairs[:].bitcast(F32).rearrange("p (u c) -> p c u", u=2)[:, cells, :],
             )
             return grouped
 

@@ -52,12 +52,12 @@ def tile_picked_bev_max_p_kernel(
         w2_raw = keep.tile([P, PACK, H], F32)
 
         near_windows = [keep.tile([P, 2 * CELLS], F32, align_bytes=64, name="near_window%d" % s) for s in range(3)]
-        far_windows = [keep.tile([P, CELLS + V], F32, name="far_window%d" % s) for s in range(2)]
+        far_windows = [keep.tile([P, CELLS], F32, name="far_window%d" % s) for s in range(2)]
         last_window = keep.tile([P, 2 * CELLS], F32)
         last_partner = keep.tile([P, 2 * CELLS], F32)
         near_pair = keep.tile([P, 2 * CELLS], F32)
         near_plane = (
-            last_partner[:, CELLS:], last_window[:, CELLS:], near_pair[:, :CELLS], near_pair[:, CELLS:]
+            last_partner[:, :CELLS], last_window[:, CELLS:], near_pair[:, :CELLS], near_pair[:, CELLS:]
         )
 
         nc.vector.memset(x_plane[:].bitcast(I32), 0)
@@ -65,7 +65,7 @@ def tile_picked_bev_max_p_kernel(
         nc.vector.memset(near_windows[0][:, :CELLS], 0.0)
         nc.vector.memset(near_windows[1][:, :CELLS], 0.0)
         nc.vector.memset(w3_plane[:].bitcast(I32), 0)
-        for cleared in (near_windows[2][:, :CELLS], far_windows[1][:, :CELLS], last_partner[:, :CELLS], last_window[:, :CELLS]):
+        for cleared in (near_windows[2][:, :CELLS], far_windows[1][:, :CELLS], last_window[:, :CELLS]):
             nc.scalar.activation(out=cleared, in_=far_windows[0][:, :CELLS], func=RELU)
 
         nc.sync.dma_start(offs_sb[:], offs)
@@ -123,13 +123,31 @@ def tile_picked_bev_max_p_kernel(
         def own_tile(name):
             return keep.tile([P, V], F32, name=name)[:]
 
-        def near_tile(g, hidden, weights, col):
-            layer_tile(hidden, weights, col, near_words, 0)
-            window = near_windows[g % len(near_windows)]
+        def scatter_near(hidden, window):
             nc.vector.tensor_copy(window[:].indirect(near_sb[:]), hidden)
-            for t in (3, 2, 0, 1):
-                nc.sync.dma_start(out=near_plane[t][QUAD * g : QUAD * (g + 1), :], in_=window[t:P:PACK, :CELLS])
 
+        def plain_near_tile(g, weights):
+            hidden = own_tile("near_hidden%d" % g)
+            layer_tile(hidden, weights, 0, near_words, 0)
+            scatter_near(hidden, near_windows[g])
+            for t in (3, 2, 0, 1):
+                nc.sync.dma_start(
+                    out=near_plane[t][QUAD * g : QUAD * (g + 1), :], in_=near_windows[g][t:P:PACK, :CELLS]
+                )
+
+        def place_upper_half(window, low_plane):
+            for h in (1, 0):
+                nc.sync.dma_start(
+                    out=near_plane[low_plane + h][half:, :], in_=window[h * half : (h + 1) * half, :CELLS]
+                )
+
+        def round_dealt(grouped, raw, lo, hi):
+            nc.scalar.copy(
+                out=grouped.rearrange("p (t m j) -> p m j t", t=PACK, j=PACK)[:, lo:hi],
+                in_=raw[:].rearrange("p j (m t) -> p m j t", t=PACK)[:, lo:hi],
+            )
+
+        half = P // 2
         near_words = pick_words(0, "near_words")
         first_grouped = keep.tile([P, PACK * P], BF16, align_bytes=64, tag="first_grouped")
         round_w1(0, first_grouped[:])
@@ -138,28 +156,28 @@ def tile_picked_bev_max_p_kernel(
 
         round_w1(1, spare(near_windows[0], P))
         w1_second = quantise("w1_second", spare(near_windows[0], P), P)
-        near_tile(0, own_tile("near_hidden0"), w1_first, 0)
+        plain_near_tile(0, w1_first)
 
-        round_w1(2, spare(near_windows[1], 2 * P))
+        round_dealt(spare(near_windows[1], 2 * P), w1_raw[2], 0, half)
         w1_rest = quantise("w1_rest", spare(near_windows[1], 2 * P), 2 * P)
-        near_tile(1, own_tile("near_hidden1"), w1_second, 0)
+        plain_near_tile(1, w1_second)
 
-        near_tile(2, own_tile("near_hidden2"), w1_rest, 0)
-
-        w2_grouped = spare(near_windows[0], H)
-        half = P // 2
+        w2_grouped = spare(near_windows[2], H)
         for lo in (0, half):
-            nc.scalar.copy(
-                out=w2_grouped.rearrange("p (t m j) -> p m j t", t=PACK, j=PACK)[:, lo : lo + half],
-                in_=w2_raw[:].rearrange("p j (m t) -> p m j t", t=PACK)[:, lo : lo + half],
-            )
+            round_dealt(w2_grouped, w2_raw, lo, lo + half)
+        near_high, near_low = w2_raw[:, 0, :], w2_raw[:, 1, :]
+        layer_tile(near_high, w1_rest, P, near_words, 0)
+        layer_tile(near_low, w1_rest, 0, near_words, 0)
         w2_mx = quantise("w2", w2_grouped, H)
-        near_tile(3, far_windows[1][:, CELLS:], w1_rest, P)
+        scatter_near(near_high, near_windows[2])
+        place_upper_half(near_windows[2], 2)
 
-        far_hidden = {3: far_windows[0][:, CELLS:]}
-        for t in (2, 1, 0):
-            far_hidden[t] = own_tile("far_hidden%d" % t)
-        for t in (3, 2, 1, 0):
+        far_hidden = {
+            3: near_windows[0][:, CELLS : CELLS + V],
+            2: own_tile("far_hidden2"),
+            1: own_tile("far_hidden1"),
+        }
+        for t in (3, 2, 1):
             layer_tile(far_hidden[t], w2_mx, t * P, far_words, 1)
 
         starts = [sum(CELL_CHUNKS[:n]) for n in range(len(CELL_CHUNKS))]
@@ -167,10 +185,11 @@ def tile_picked_bev_max_p_kernel(
         pair_view = pairs[:].rearrange("p (u c e) -> p u c e", u=2, e=2)
 
         halves = (slice(0, CELLS // 2), slice(CELLS // 2, CELLS))
-        for t in (3, 2):
-            window = far_windows[t % 2]
+
+        def scatter_far(t, window):
             nc.vector.tensor_copy(window[:].indirect(far_sb[:]), far_hidden[t])
-            difference = keep.tile([P, CELLS], F32, name="difference%d" % t)
+
+        def join_off_vector(t, window, difference):
             excess = keep.tile([P, CELLS], F32, name="excess%d" % t)
             for cells in halves:
                 nc.gpsimd.tensor_tensor(difference[:, cells], window[:, cells], near_plane[t][:, cells], ALU.subtract)
@@ -179,8 +198,19 @@ def tile_picked_bev_max_p_kernel(
                 nc.gpsimd.tensor_tensor(
                     pair_view[:, 1, cells, t % 2], near_plane[t][:, cells], excess[:, cells], ALU.add
                 )
-        nc.vector.tensor_copy(last_partner[:].indirect(far_sb[:]), far_hidden[1])
-        nc.vector.tensor_copy(last_window[:].indirect(far_sb[:]), far_hidden[0])
+
+        scatter_far(3, far_windows[1])
+        scatter_near(near_low, near_windows[0])
+        place_upper_half(near_windows[0], 0)
+        difference = keep.tile([P, CELLS], F32, tag="difference")
+        join_off_vector(3, far_windows[1], difference[:])
+        far_hidden[0] = keep.tile([P, V], F32, name="far_hidden0", tag="difference")[:]
+        layer_tile(far_hidden[0], w2_mx, 0, far_words, 1)
+        scatter_far(2, far_windows[0])
+        join_off_vector(2, far_windows[0], last_partner[:, CELLS:])
+        scatter_far(1, far_windows[1])
+        nc.scalar.copy(out=last_partner[:, CELLS:], in_=far_windows[1][:])
+        scatter_far(0, last_window)
 
         out_rows = out.rearrange("(m p) c -> p m c", p=P)
 
@@ -189,7 +219,7 @@ def tile_picked_bev_max_p_kernel(
             nc.vector.tensor_tensor(
                 pair_view[:, 0, cells, :],
                 last_window[:].rearrange("p (e c) -> p c e", e=2)[:, cells, :],
-                last_partner[:].rearrange("p (e c) -> p c e", e=2)[:, cells, ::-1],
+                last_partner[:].rearrange("p (e c) -> p c e", e=2)[:, cells, :],
                 ALU.max,
             )
             grouped = keep.tile([P, PACK * CELL_CHUNKS[n]], BF16, align_bytes=64, name="z_grouped%d" % n)

from contextlib import ExitStack

import concourse.mybir as mybir

K, T, H, N, CELLS, V = 512, 2048, 512, 256, 1024, 512
FLOPS = 2 * (2 * K * H * V + H * N * CELLS)

F32 = mybir.dt.float32
BF16 = mybir.dt.bfloat16
I32 = mybir.dt.int32
U32 = mybir.dt.uint32
U16 = mybir.dt.uint16
U8 = mybir.dt.uint8
FP8X4 = mybir.dt.float8_e4m3fn_x4
RELU = mybir.ActivationFunctionType.Relu
ALU = mybir.AluOpType

P = 128
PACK = 4
QUAD = 32
LIST_ROWS = 16
CELL_CHUNKS = (256, 256, 256, 128, 128)


def load_scale_rows(nc, plane, rows):
    for q in range(P // QUAD):
        nc.sync.dma_start(
            out=plane[QUAD * q : QUAD * q + PACK, :].bitcast(I32),
            in_=rows[PACK * q : PACK * (q + 1), :].bitcast(I32),
        )


def tile_picked_bev_max_p_kernel(
    tc, x_words, x_scales, w1, w2, w3_words, w3_scales, offs, near, far, out
):
    nc = tc.nc
    with ExitStack() as ctx:
        keep = ctx.enter_context(tc.tile_pool(name="keep", bufs=1))
        layer_psum = ctx.enter_context(tc.psum_pool(name="layer_psum", bufs=4))
        out_psum = ctx.enter_context(tc.psum_pool(name="out_psum", bufs=4))

        offs_sb = keep.tile([P, 2 * V // LIST_ROWS], U16)
        near_sb = keep.tile([P, V // LIST_ROWS], U16)
        far_sb = keep.tile([P, V // LIST_ROWS], U16)

        x_plane = keep.tile([P, T], U8, align_bytes=64)
        x_table = keep.tile([P, T], I32, align_bytes=64)
        w3_plane = keep.tile([P, N], U8, align_bytes=64)
        w3_codes = keep.tile([P, N], I32, align_bytes=64)
        w1_spans = ((0, P), (P, 2 * P), (2 * P, H))
        w1_raw = [keep.tile([P, PACK, hi - lo], F32, name="w1_raw%d" % s) for s, (lo, hi) in enumerate(w1_spans)]
        w2_raw = keep.tile([P, PACK, H], F32)

        near_windows = [keep.tile([P, 2 * CELLS], F32, align_bytes=64, name="near_window%d" % s) for s in range(3)]
        far_windows = [keep.tile([P, CELLS], F32, name="far_window%d" % s) for s in range(2)]
        last_window = keep.tile([P, 2 * CELLS], F32)
        last_partner = keep.tile([P, 2 * CELLS], F32)
        near_pair = keep.tile([P, 2 * CELLS], F32)
        near_plane = (
            last_partner[:, :CELLS], last_window[:, CELLS:], near_pair[:, :CELLS], near_pair[:, CELLS:]
        )

        nc.vector.memset(x_plane[:].bitcast(I32), 0)
        nc.vector.memset(far_windows[0][:, :CELLS], 0.0)
        nc.vector.memset(near_windows[0][:, :CELLS], 0.0)
        nc.vector.memset(near_windows[1][:, :CELLS], 0.0)
        nc.vector.memset(w3_plane[:].bitcast(I32), 0)
        for cleared in (near_windows[2][:, :CELLS], far_windows[1][:, :CELLS], last_window[:, :CELLS]):
            nc.scalar.activation(out=cleared, in_=far_windows[0][:, :CELLS], func=RELU)

        nc.sync.dma_start(offs_sb[:], offs)
        nc.sync.dma_start(near_sb[:], near)
        nc.sync.dma_start(far_sb[:], far)
        load_scale_rows(nc, x_plane, x_scales[0])
        nc.sync.dma_start(out=x_table[:], in_=x_words[0].rearrange("p n t -> p (n t)").bitcast(I32))
        w1_rows = w1.rearrange("(p j) c -> p j c", j=PACK)
        for s, (lo, hi) in enumerate(w1_spans):
            nc.sync.dma_start(out=w1_raw[s][:], in_=w1_rows[:, :, lo:hi])
        nc.sync.dma_start(out=w2_raw[:], in_=w2.rearrange("(p j) c -> p j c", j=PACK))
        nc.sync.dma_start(out=w3_codes[:], in_=w3_words[0].rearrange("p n t -> p (n t)").bitcast(I32))
        load_scale_rows(nc, w3_plane, w3_scales[0])

        picked_bytes = keep.tile([P, 2 * V], U8, align_bytes=64)
        nc.vector.tensor_copy(picked_bytes[:], x_plane[:].indirect(offs_sb[:]))

        def pick_words(sensor, tag):
            words = keep.tile([P, V], U32, align_bytes=64, name="picked_words%d" % sensor, tag=tag)
            cols = V // LIST_ROWS
            nc.vector.tensor_copy(
                words[:], x_table[:].bitcast(U32).indirect(offs_sb[:, sensor * cols : (sensor + 1) * cols])
            )
            return words

        def quantise(name, grouped, width):
            codes = keep.tile([P, width], U32, align_bytes=64, name=name + "_codes")
            plane = keep.tile([P, width], U8, align_bytes=64, name=name + "_plane")
            nc.vector.quantize_mx(out=codes[:].bitcast(FP8X4), scales=plane[:], in_=grouped)
            return codes, plane

        def round_w1(s, grouped):
            nc.scalar.copy(
                out=grouped.rearrange("p (c i j) -> p c j i", i=PACK, j=PACK),
                in_=w1_raw[s][:].rearrange("p j (c i) -> p c j i", i=PACK),
            )

        def spare(window, width):
            return window[:, CELLS : CELLS + width * PACK // 2].bitcast(BF16)

        def layer_tile(hidden, weights, col, words, sensor):
            codes, plane = weights
            acc = layer_psum.tile([P, V], F32, tag="layer")
            nc.tensor.matmul_mx(
                out=acc[:],
                lhsT=codes[:, col : col + P].bitcast(FP8X4),
                lhsT_scale=plane[:, col : col + P],
                rhs=words[:].bitcast(FP8X4),
                rhs_scale=picked_bytes[:, sensor * V : (sensor + 1) * V],
                start=True,
                stop=True,
            )
            nc.scalar.activation(out=hidden, in_=acc[:], func=RELU)

        def own_tile(name):
            return keep.tile([P, V], F32, name=name)[:]

        def scatter_near(hidden, window):
            nc.vector.tensor_copy(window[:].indirect(near_sb[:]), hidden)

        def plain_near_tile(g, weights):
            hidden = own_tile("near_hidden%d" % g)
            layer_tile(hidden, weights, 0, near_words, 0)
            scatter_near(hidden, near_windows[g])
            for t in (3, 2, 0, 1):
                nc.sync.dma_start(
                    out=near_plane[t][QUAD * g : QUAD * (g + 1), :], in_=near_windows[g][t:P:PACK, :CELLS]
                )

        def place_upper_half(window, low_plane):
            for h in (1, 0):
                nc.sync.dma_start(
                    out=near_plane[low_plane + h][half:, :], in_=window[h * half : (h + 1) * half, :CELLS]
                )

        def round_dealt(grouped, raw, lo, hi):
            nc.scalar.copy(
                out=grouped.rearrange("p (t m j) -> p m j t", t=PACK, j=PACK)[:, lo:hi],
                in_=raw[:].rearrange("p j (m t) -> p m j t", t=PACK)[:, lo:hi],
            )

        half = P // 2
        near_words = pick_words(0, "near_words")
        first_grouped = keep.tile([P, PACK * P], BF16, align_bytes=64, tag="first_grouped")
        round_w1(0, first_grouped[:])
        w1_first = quantise("w1_first", first_grouped[:], P)
        far_words = pick_words(1, "first_grouped")

        round_w1(1, spare(near_windows[0], P))
        w1_second = quantise("w1_second", spare(near_windows[0], P), P)
        plain_near_tile(0, w1_first)

        round_dealt(spare(near_windows[1], 2 * P), w1_raw[2], 0, half)
        w1_rest = quantise("w1_rest", spare(near_windows[1], 2 * P), 2 * P)
        plain_near_tile(1, w1_second)

        w2_grouped = spare(near_windows[2], H)
        for lo in (0, half):
            round_dealt(w2_grouped, w2_raw, lo, lo + half)
        near_high, near_low = w2_raw[:, 0, :], w2_raw[:, 1, :]
        layer_tile(near_high, w1_rest, P, near_words, 0)
        layer_tile(near_low, w1_rest, 0, near_words, 0)
        w2_mx = quantise("w2", w2_grouped, H)
        scatter_near(near_high, near_windows[2])
        place_upper_half(near_windows[2], 2)

        far_hidden = {
            3: near_windows[0][:, CELLS : CELLS + V],
            2: own_tile("far_hidden2"),
            1: own_tile("far_hidden1"),
        }
        for t in (3, 2, 1):
            layer_tile(far_hidden[t], w2_mx, t * P, far_words, 1)

        starts = [sum(CELL_CHUNKS[:n]) for n in range(len(CELL_CHUNKS))]
        pairs = keep.tile([P, PACK * CELLS], BF16)
        pair_view = pairs[:].rearrange("p (u c e) -> p u c e", u=2, e=2)

        halves = (slice(0, CELLS // 2), slice(CELLS // 2, CELLS))

        def scatter_far(t, window):
            nc.vector.tensor_copy(window[:].indirect(far_sb[:]), far_hidden[t])

        def join_off_vector(t, window, difference):
            excess = keep.tile([P, CELLS], F32, name="excess%d" % t)
            for cells in halves:
                nc.gpsimd.tensor_tensor(difference[:, cells], window[:, cells], near_plane[t][:, cells], ALU.subtract)
                nc.scalar.activation(out=excess[:, cells], in_=difference[:, cells], func=RELU)
            for cells in halves:
                nc.gpsimd.tensor_tensor(
                    pair_view[:, 1, cells, t % 2], near_plane[t][:, cells], excess[:, cells], ALU.add
                )

        scatter_far(3, far_windows[1])
        scatter_near(near_low, near_windows[0])
        place_upper_half(near_windows[0], 0)
        difference = keep.tile([P, CELLS], F32, tag="difference")
        join_off_vector(3, far_windows[1], difference[:])
        far_hidden[0] = keep.tile([P, V], F32, name="far_hidden0", tag="difference")[:]
        layer_tile(far_hidden[0], w2_mx, 0, far_words, 1)
        scatter_far(2, far_windows[0])
        join_off_vector(2, far_windows[0], last_partner[:, CELLS:])
        scatter_far(1, far_windows[1])
        nc.scalar.copy(out=last_partner[:, CELLS:], in_=far_windows[1][:])
        scatter_far(0, last_window)

        out_rows = out.rearrange("(m p) c -> p m c", p=P)

        def weave(n):
            cells = slice(starts[n], starts[n] + CELL_CHUNKS[n])
            nc.vector.tensor_tensor(
                pair_view[:, 0, cells, :],
                last_window[:].rearrange("p (e c) -> p c e", e=2)[:, cells, :],
                last_partner[:].rearrange("p (e c) -> p c e", e=2)[:, cells, :],
                ALU.max,
            )
            grouped = keep.tile([P, PACK * CELL_CHUNKS[n]], BF16, align_bytes=64, name="z_grouped%d" % n)
            nc.scalar.copy(
                out=grouped[:].bitcast(F32).rearrange("p (c u) -> p c u", u=2),
                in_=pairs[:].bitcast(F32).rearrange("p (u c) -> p c u", u=2)[:, cells, :],
            )
            return grouped

        def last_layer(n, grouped):
            lo, width = starts[n], CELL_CHUNKS[n]
            codes, plane = quantise("z%d" % n, grouped[:], width)
            acc = out_psum.tile([P, N // P, width], F32, tag="last")
            for m in range(N // P):
                nc.tensor.matmul_mx(
                    out=acc[:, m, :],
                    lhsT=w3_codes[:, m * P : (m + 1) * P].bitcast(FP8X4),
                    lhsT_scale=w3_plane[:, m * P : (m + 1) * P],
                    rhs=codes[:].bitcast(FP8X4),
                    rhs_scale=plane[:],
                    start=True,
                    stop=True,
                )
            return acc

        def store(n, acc):
            lo, width = starts[n], CELL_CHUNKS[n]
            result = keep.tile([P, N // P, width], F32, name="result%d" % n)
            if n % 2 == 0:
                nc.scalar.copy(out=result[:], in_=acc[:])
            else:
                nc.vector.tensor_copy(out=result[:], in_=acc[:])
            nc.sync.dma_start(out=out_rows[:, :, lo : lo + width], in_=result[:])

        count = len(CELL_CHUNKS)
        woven, sums = {}, {}
        for step in range(count + 3):
            if step < count:
                woven[step] = weave(step)
            if 0 <= step - 2 < count:
                sums[step - 2] = last_layer(step - 2, woven[step - 2])
            if 0 <= step - 3 < count:
                store(step - 3, sums[step - 3])
